import numpy as np, ml_dtypes
CORES = [9,25,41,57]
N = 4
BF = ml_dtypes.bfloat16
W, C, K, VISITS = 4096, 1024, 256, 5
LEV = np.arange(16).reshape(1, 1, 16, 1)
HC = 39 + 14 * LEV
UC = 5 + 10 * LEV
SIZES = np.array([1, 1, 2, 2, 3, 4, 6, 8, 16, 32, 64, 128, 256, 512, W, W]).reshape(1, 1, 16, 1)
def take(a, i):
    return np.take_along_axis(a, i, a.ndim - 1)
def cell(z):
    return (255 + np.add.reduce(HC * z, axis=2)) & (C - 1)
def first(keys):
    return np.unique(keys, return_index=True)[1]
def parts(rng, amp=12):
    pool = np.argsort(rng.random((8, 16, W)), axis=-1); pl = np.broadcast_to(pool[None], (N, 8, 16, W))
    fo = np.where(rng.random((N, 8, W)) < 0.6, np.arange(W), rng.integers(0, W, (N, 8, W)))
    la = take(pl, (rng.random((N, 8, 16, K)) * SIZES).astype(np.int64)); bk = take(pl, (rng.random((N, 8, 16, C)) * SIZES).astype(np.int64))
    cen = rng.integers(40, 216, (1, 8, 16, 1))
    far = rng.random((N, 8, 1, W)) < 0.06
    for q in range(N):
        for g in range(8):
            far[q, g, 0, fo[q, g, pool[g, :4, :2].reshape(-1)]] = False
    x = np.where(far, rng.integers(0, 256, (N, 8, 16, W)), cen + rng.integers(-amp, amp + 1, (N, 8, 16, W)))
    z = np.where(rng.random((N, 8, 1, K)) < 0.04, rng.integers(0, 256, (N, 8, 16, K)), cen + rng.integers(-amp, amp + 1, (N, 8, 16, K)))
    t = 235 - 4 * LEV + rng.integers(0, 4, (N, 8, 16, 1))
    c = cell(z); same = rng.random((N, 8, K)) < 0.15
    for q in range(N):
        for g in range(8):
            j = np.flatnonzero(same[q, g]); j = j[first(c[q, g, j])]
            bk[q, g][:, c[q, g, j]] = la[q, g][:, j]
    return x, fo, bk, la, z, t
def pack(x, fo, bk, la, z, t):
    return {"x": np.ascontiguousarray(x.reshape(N, 128, W)).astype(np.float32).astype(BF), "fw": np.ascontiguousarray(fo).astype(np.int32),
            "bk": np.ascontiguousarray(bk.reshape(N, 128, C)).astype(np.int32), "la": np.ascontiguousarray(la.reshape(N, 128, K)).astype(np.int32),
            "zz": np.ascontiguousarray(z.reshape(N, 128, K)).astype(np.float32).astype(BF), "th": np.ascontiguousarray(t.reshape(N, 128, 1)).astype(np.int32)}
def setup_inputs(rng):
    return pack(*parts(rng))
def setup_inputs_spread(rng):
    x = np.minimum((np.exp2(8 * rng.random((N, 8, 1, W))) * rng.random((N, 8, 16, W))).astype(np.int64), 255)
    z = np.minimum((np.exp2(8 * rng.random((N, 8, 1, K))) * rng.random((N, 8, 16, K))).astype(np.int64), 255)
    t = -np.sort(-np.minimum(np.exp2(12 * rng.random((N, 8, 16, 1))).astype(np.int64), 4080), axis=2)
    fo = rng.integers(0, W, (N, 8, W)); la = (W * rng.random((N, 8, 16, K)) ** 3).astype(np.int64); bk = (W * rng.random((N, 8, 16, C)) ** 3).astype(np.int64)
    return pack(x, fo, np.minimum(bk, W - 1), np.minimum(la, W - 1), z, t)
def setup_inputs_ends(rng):
    def both(n):
        k = rng.integers(0, 3, (N, 8, 1, n)); return np.where(k == 0, 0, np.where(k == 1, 255, 255 * rng.integers(0, 2, (N, 8, 16, n))))
    x, z = both(W), both(K)
    fo = (W - 1) * rng.integers(0, 2, (N, 8, W)); bk = (W - 1) * rng.integers(0, 2, (N, 8, 16, C)); la = (W - 1) * rng.integers(0, 2, (N, 8, 16, K))
    t = 4080 * (rng.random((N, 8, 16, 1)) < rng.choice(np.array([0.5, 0.8, 0.95]), (N, 8, 1, 1))).astype(np.int64)
    t[N - 1, 7] = 4080; t[:, 6] = 4080; t[:, 6, 15] = 0
    near = (255 * (16 - np.arange(16) // 2) - 1 + np.arange(16) % 2).reshape(16, 1)
    for g, o in ((3, 1), (5, -1)):
        z[:, g] = 255 * (np.argsort(rng.random((N, 16, K)), axis=1) < np.argsort(rng.random((N, 1, K)), axis=-1) % 17)
        t[:, g] = near[::o]
    x[:, 1::2, :, 0] = 0; x[:, 1::2, :, W - 1] = 255; fo[:, 1::2, 0] = 0; fo[:, 1::2, W - 1] = W - 1
    z[..., K - 1] = 0; la[..., K - 1] = W - 1; z[..., K - 2] = 255; la[..., K - 2] = 0
    bk[:, 1::2, :, 255] = 0; bk[:, 1::2, :, C - 1] = W - 1
    return pack(x, fo, bk, la, z, t)
def setup_inputs_corners(rng):
    x, fo, bk, la, z, t = parts(rng); a = np.arange(W)
    pat = [a, 0 * a, 0 * a + W - 1, np.maximum(a - 1, 0), W - 1 - a, (a + 1) % W, a ^ 1]
    kind = rng.integers(0, 4, (N, 8)); kind[0] = (1, 0, 2, 3, 1, 3, 0, 1)
    r = rng.random((N, 8, 1, K)); la = np.where(r < 0.1, 0, np.where(r < 0.2, W - 1, la))
    z[..., K - 1] = z[..., 0]; c = cell(z)
    for q in range(N):
        for g in range(8):
            i = (g + q) % 8
            if i < 7: fo[q, g] = pat[i]
            if kind[q, g] == 1: t[q, g] = 4080
            if kind[q, g] == 2: t[q, g] = 0
            if kind[q, g] == 3: t[q, g] = np.where(LEV[0, 0] < rng.integers(1, 16), 4080, 0)
            for j in rng.permutation(K)[:8]:
                bk[q, g][:, c[q, g, j]] = la[q, g][:, j]; bk[q, g, 15, c[q, g, j]] = rng.integers(0, W)
    return pack(x, fo, bk, la, z, t)
def setup_inputs_crowd(rng):
    x, fo, bk, la, z, t = parts(rng)
    for q in range(N):
        for g in range(8):
            k = g % 4; j = K - 1 if q == 0 else int(rng.integers(0, K))
            if k != 3: z[q, g] = z[q, g][:, :1].copy(); la[q, g] = la[q, g][:, :1].copy()
            if k == 2: t[q, g] = 0
            else: fo[q, g] = np.arange(W); la[q, g, 0] = W - 1; t[q, g, 0] = 4080
            c = (255 + np.add.reduce(HC[0, 0] * z[q, g], axis=0)) & (C - 1)
            if k in (0, 1): bk[q, g][:, c[0]] = la[q, g][:, 0]; bk[q, g, 0, c[0]] = rng.integers(0, W - 1)
            if k == 3: bk[q, g, 0] = rng.integers(0, W - 1, C)
            if k == 1 or (k == 3 and q % 2 == 1): la[q, g][:, j] = bk[q, g][:, c[j]]
    return pack(x, fo, bk, la, z, t)
def setup_inputs_ties(rng):
    x, fo, bk, la, z, t = parts(rng, 1)
    t = -np.sort(-rng.integers(14, 25, (N, 8, 16, 1)), axis=2)
    for g in (2, 6):
        mid = rng.integers(40, 216, (16, 1)); fo[:, g] = np.arange(W)
        x[:, g] = mid + rng.integers(-1, 2, (N, 16, W)); z[:, g] = mid + rng.integers(-1, 2, (N, 16, K))
    t[:, 2] = 22 - LEV[0, 0] // 2
    for q in range(N):
        a = rng.integers(0, W - 1, (16, 1)); la[q, 2] = a; bk[q, 2] = a
        x[q, 2, :, W - 1] = x[q, 2, :, int(a[0, 0])]
        j = rng.permutation(K)[:1 + q % 3]; la[q, 2, 0, j] = W - 1; z[q, 2][:, j] = x[q, 2, :, W - 1:]
    la[:, 6] = rng.integers(0, W, (N, 16, K)); bk[:, 6] = rng.integers(0, W, (N, 16, C)); t[:, 6] = 9
    return pack(x, fo, bk, la, z, t)
def check_inputs(d):
    bad = []
    for k, hi in (("x", 255), ("fw", W - 1), ("bk", W - 1), ("la", W - 1), ("zz", 255), ("th", 4080)):
        v = np.asarray(d[k]).astype(np.float64)
        if not (np.min(v) >= 0 and np.max(v) <= hi): bad.append("range of " + k)
        elif np.any(v != np.floor(v)): bad.append("whole numbers of " + k)
    return bad
def reference(x, fw, bk, la, zz, th):
    X = x.astype(np.float32).astype(np.int32).reshape(N, 8, 16, W); Z = zz.astype(np.float32).astype(np.int32).reshape(N, 8, 16, K)
    F = fw.astype(np.int64).reshape(N, 8, W); B = bk.astype(np.int64).reshape(N, 8, 16, C); L = la.astype(np.int64).reshape(N, 8, 16, K)
    T = th.astype(np.int64).reshape(N, 8, 16, 1); A = np.zeros((N, 8, 1, 1), np.int64)
    for v in range(VISITS):
        if v > 0:
            s = 1 + (v - 1) % (N - 1); L = np.roll(L, s, axis=0); Z = np.roll(Z, s, axis=0)
        L = take(F, L.reshape(N, 8, 16 * K)).reshape(N, 8, 16, K)
        c = cell(Z)
        G = take(F, take(B, c[:, :, None, :]).reshape(N, 8, 16 * K)).reshape(N, 8, 16, K)
        d = np.add.reduce(np.abs(take(X, L.reshape(N, 8, 1, 16 * K)).reshape(N, 8, 16, 16, K) - Z[:, :, :, None, :]), axis=2)
        e = np.add.reduce(np.abs(take(X, G.reshape(N, 8, 1, 16 * K)).reshape(N, 8, 16, 16, K) - Z[:, :, :, None, :]), axis=2)
        fail = d > T + (A & 15); ks = np.where(np.any(fail, axis=2), np.argmax(fail, axis=2), 16)
        good = (G != L) & (e <= T); m = np.where(np.any(good, axis=2), np.argmax(good, axis=2), 16)
        merge = m < ks
        u = ((255 + np.add.reduce(UC * Z, axis=2)) & 1023)[:, :, None, :]
        new = np.where(LEV >= ks[:, :, None, :], (((L * u) >> 5) + L + 613 * LEV) & (W - 1), L)
        w = np.take_along_axis(new, np.minimum(ks, 15)[:, :, None, :], 2)
        val = np.where(ks[:, :, None, :] < 16, Z, (take(X, w) + Z) >> 1)
        mm = np.minimum(m, 15)[:, :, None, :]; gm = np.take_along_axis(G, mm, 2); lm = np.take_along_axis(L, mm, 2)
        hi = np.maximum(gm, lm)[:, :, 0]; lo = np.minimum(gm, lm)[:, :, 0]
        Z = np.where(m[:, :, None, :] < 16, (Z + take(X, gm)) >> 1, Z)
        for q in range(N):
            for g in range(8):
                j = first(w[q, g, 0]); X[q, g][:, w[q, g, 0, j]] = val[q, g][:, j]
                j = first(c[q, g]); B[q, g][:, c[q, g, j]] = new[q, g][:, j]
                j = np.flatnonzero(merge[q, g]); j = j[first(hi[q, g, j])]; F[q, g, hi[q, g, j]] = lo[q, g, j]
        A = np.add.reduce(merge.astype(np.int64), axis=2)[:, :, None, None]
        L = new
    return {"yx": X.reshape(N, 128, W).astype(np.float32).astype(BF), "yf": F.astype(np.float32), "yb": B.reshape(N, 128, C).astype(np.float32),
            "yl": L.reshape(N, 128, K).astype(np.float32), "yz": Z.reshape(N, 128, K).astype(np.float32).astype(BF)}

@@ -1,0 +1,513 @@
+from concourse.mybir import AluOpType as A, ActivationFunctionType as AF
+
+VIS, W, C, K, LV = 5, 4096, 1024, 256, 16
+PAD = 16
+NCH = 4
+CL = K // NCH
+CE = CL * LV
+BASE = ("fg0 fg1 fg2 fg3 zb sc eb xl0 ul0 xl1 ul1 fh0 xl2 ul2 ob fh1 xl3 ul3 fh2 fh3 flf xg0 da0 da1 ug0 xg1 ug1 xg2 sd0 da2 ug2 "
+        "xg3 sd1 sd2 da3 sd3 df nn ea0 ug3 nw ea1 ea2 ea3 wv wm se0 se1 hv we ")
+ORDER = BASE + "sl bs vv se2 se3 eg h1 hk l1 zi h2 wl lm zz h3 wo xs aa l2 h4 fs"
+ORDER_LAST = BASE + "sl wl vv wo xs se2 se3 eg h1 hk l1 ff0 zi h2 ff1 lm zz h3 ff2 ff3 bs h4 fs"
+
+SCRATCH, LOC = {}, {}
+for _b, _d, _l in (
+        ("", "bfloat16", "X 4112 Fw 4112 FG 4096 FH 4096 D 4096 E 4096 DA 4096 EA 4096 z16 4096 zsp 4096 zm 4096 fh 256 fl 256 eq 256 "
+         "fs 256 gs 256 fg 256 mg 256 Emb 256 Emw 256 Emh 256 val 256 hm 256 lod 256"),
+        ("kb", "bfloat16", "SK 2048 MK 2048 cS 128 cSr 128 cSn 128 cSb 128 cSbn 128 cS1 128 cS4 128 cS4n 128 cSq 128 cI 128 cI8 128 C1 128 "
+         "C2 128 C2f 128 C3 128 C4 128 c01 128 cZ 128 MSK 256 dd 32 J16 16 ones 256"),
+        ("", "float32", "Ff 4112 Aac 1 fc 256 FLc 256 FLf 256 r1 256 lof 256 ybo 1024 ylo 256"),
+        ("kf", "float32", "cSf 128 mask 256 rq 128 gq 128 code 128 tr 128 idn 128 tmp 128 tmp2 128 rq2 256 s16 16 s8 16 j16 16 rp 1 "
+         "gp 1 m0 1 m1 1 m15 1 zc 1 zc2 1 zc3 1 c613 1 bY 1 bG 1 bM 1 Tn 1 Tp 1 thr 1"),
+        ("", "int32", "Bt 1040 tI 1 f0 256 la0 256 i1 256 i2 256 r2 256 sn 256 new 256 zh 256 hd 256"),
+        ("ki", "int32", "pi 1 pi2 1 pi3 1 a1 1 a2 1"),
+        ("", "float16", "bu 256 nC 256 Vw 256 Vh 256 Vl 256 WTb 256 WTw 256 WTh 256"),
+        ("", "uint16", "bl 16 Bb 256 FLu 256 Gu 256 ofb 32 ofw 32 ofh 32 idx 16")):
+    _l, _c = _l.split(), 0
+    for _i in range(0, len(_l), 2):
+        _n, _w = _l[_i], int(_l[_i + 1])
+        if _b:
+            LOC[_n] = (_b, _c, _w)
+            _c += (_w + 15) // 16 * 16
+            SCRATCH[_b] = ("sbuf", [128, _c], _d)
+        else:
+            SCRATCH[_n] = ("sbuf", [128, _w], _d)
+for _v in range(VIS + 1):
+    if _v < VIS:
+        SCRATCH["L%d" % _v] = ("sbuf", [128, K], "uint16")
+        SCRATCH["z%d" % _v] = ("sbuf", [128, K], "bfloat16")
+    if _v > 0:
+        SCRATCH["zs%d" % _v] = ("sbuf", [128, K], "bfloat16")
+    if 0 < _v < VIS:
+        SCRATCH["Ls%d" % _v] = ("sbuf", [128, K], "uint16")
+PSUM = {"pF": 1024, "pd": 512, "pe": 512, "pC": 512, "pS": 512, "pH": 512, "pX": 512}
+for _n in PSUM:
+    SCRATCH[_n] = ("psum", [128, PSUM[_n]], "float32")
+NDMA = 16
+SEMAPHORES = ["q_v", "q_s", "q_t", "q_g"] + ["d%d" % i for i in range(NDMA)]
+for _v in range(1, VIS):
+    SEMAPHORES += ["aL%d" % _v, "aZ%d" % _v, "lL%d" % _v, "lZ%d" % _v]
+
+
+def make(g, T):
+    queues = {"v": g.vector, "s": g.scalar, "t": g.tensor, "g": g, "y": g.sync}
+    n = {"v": 0, "s": 0, "t": 0, "g": 0}
+    clk = {q: {} for q in queues}
+    snap, hist, bank, final = {}, {}, {}, {}
+    nd = [0]
+
+    def ap(o):
+        if o[0] == "@":
+            return ap(o[1]).indirect(ap(o[2]))
+        b, a = (LOC[o[0]][0], LOC[o[0]][1]) if o[0] in LOC else (o[0], 0)
+        if len(o) == 4 and o[3] != 1:
+            return T[b][:, a + o[1]:a + o[2]:o[3]]
+        return T[b][:, a + o[1]:a + o[2]]
+
+    def regs(o):
+        if o is None or isinstance(o, (int, float)):
+            return []
+        if o[0] == "@":
+            return regs(o[1]) + regs(o[2])
+        return [o]
+
+    def val(o):
+        return o if o is None or isinstance(o, (int, float)) else ap(o)
+
+    def wait(q, tok):
+        s, v = tok
+        if clk[q].get(s, 0) >= v:
+            return
+        queues[q].wait_ge(T.sem[s], v)
+        for a, b in snap.get(tok, {}).items():
+            if clk[q].get(a, 0) < b:
+                clk[q][a] = b
+        clk[q][s] = v
+
+    def banks(o):
+        return range(o[1] // 512, (o[2] - 1) // 512 + 1) if o[0] in PSUM else ()
+
+    def order(q, reads, writes, own):
+        need = {}
+
+        def want(tok):
+            if need.get(tok[0], 0) < tok[1]:
+                need[tok[0]] = tok[1]
+        for o, w in [(r, False) for r in reads] + [(r, True) for r in writes]:
+            for h in hist.get(o[0], []):
+                if h[1] <= o[1] or h[0] >= o[2] or not (w or h[4]):
+                    continue
+                if h[2] == q and own and w and (q == "t" or not h[4]):
+                    continue
+                want(h[3])
+            for b in banks(o):
+                for q2, tok in bank.get((o[0], b), {}).items():
+                    if q2 != q:
+                        want(tok)
+        for s in need:
+            wait(q, (s, need[s]))
+
+    def note(q, reads, writes, tok):
+        snap[tok] = dict(clk.get(q, {}))
+        for o, w in [(r, False) for r in reads] + [(r, True) for r in writes]:
+            h = hist.setdefault(o[0], [])
+            if w and (len(o) < 4 or o[3] == 1):
+                h[:] = [e for e in h if not (o[1] <= e[0] and e[1] <= o[2])]
+            if not w:
+                h[:] = [e for e in h if not (e[2] == q and not e[4] and o[1] <= e[0] and e[1] <= o[2] and e[3][0] == tok[0])]
+            h.append((o[1], o[2], q, tok, w))
+            for b in banks(o):
+                bank.setdefault((o[0], b), {})[q] = tok
+        final[tok[0]] = max(final.get(tok[0], 0), tok[1])
+
+    def comp(q, reads, writes, call):
+        order(q, reads, writes, True)
+        n[q] += 1
+        call(queues[q]).then_inc(T.sem["q_" + q], 1)
+        note(q, reads, writes, ("q_" + q, n[q]))
+
+    def cp(out, in_):
+        comp("v", regs(in_), regs(out), lambda e: e.tensor_copy(ap(out), ap(in_)))
+
+    def ms(out, c):
+        comp("v", [], regs(out), lambda e: e.memset(ap(out), c))
+
+    def tt(out, a, b, op):
+        comp("v", regs(a) + regs(b), regs(out), lambda e: e.tensor_tensor(ap(out), ap(a), ap(b), op))
+
+    def ts(out, a, s1, op0, s2=None, op1=None):
+        if op1 is None:
+            comp("v", regs(a) + regs(s1), regs(out), lambda e: e.tensor_scalar(ap(out), ap(a), val(s1), None, op0))
+        else:
+            comp("v", regs(a) + regs(s1) + regs(s2), regs(out), lambda e: e.tensor_scalar(ap(out), ap(a), val(s1), val(s2), op0, op1))
+
+    def scan(out, a, b, op0, op1):
+        comp("v", regs(a) + regs(b), regs(out), lambda e: e.tensor_tensor_scan(ap(out), ap(a), ap(b), 0.0, op0, op1))
+
+    def act(out, in_, func, bias=0.0, scale=1.0, acc=None):
+        kw = {}
+        if acc is not None:
+            kw["accum_out"] = ap(acc)
+        if not (isinstance(bias, float) and bias == 0.0):
+            kw["bias"] = val(bias)
+        if not (isinstance(scale, float) and scale == 1.0):
+            kw["scale"] = val(scale)
+        comp("s", regs(in_) + regs(bias) + regs(scale), regs(out) + regs(acc), lambda e: e.activation(ap(out), ap(in_), func, **kw))
+
+    def mm(out, lhsT, rhs, start=True, stop=True):
+        comp("t", regs(lhsT) + regs(rhs), regs(out), lambda e: e.matmul(ap(out), ap(lhsT), ap(rhs), start, stop))
+
+    def iota(out, pattern, mult):
+        comp("g", [], regs(out), lambda e: e.iota(ap(out), pattern, 0, mult, allow_small_or_imprecise_dtypes=True))
+
+    def pick(out, in_, pattern, base):
+        comp("g", regs(in_), regs(out), lambda e: e.affine_select(ap(out), ap(in_), pattern, A.is_equal, 0.0, base, 0))
+
+    def dma(q, out, in_, reads, writes, beside=False):
+        order(q, reads, [] if beside else writes, False)
+        s = "d%d" % nd[0]
+        nd[0] += 1
+        queues[q].dma_start(out, in_).then_inc(T.sem[s], 16)
+        note("dma", reads, [o + (2,) for o in writes] if beside else writes, (s, 16))
+        snap[(s, 16)] = dict(clk[q])
+
+    def arrive(o, s, v):
+        note("in", [], [o], (s, v))
+
+    def send(o, out, topo, core, dst, rs, ls):
+        order("g", regs(o), [], False)
+        rid, pid = topo.addr(dst)[0:2]
+        g.remote_dma(ap(out), ap(o), T.sem[rs], T.sem[ls], pid, rid, topo.mask(core, dst))
+        note("out", regs(o), [], (ls, len(topo.engines(core, dst))))
+
+    def finish():
+        for s in final:
+            wait("g", (s, final[s]))
+    return cp, ms, tt, ts, scan, act, mm, iota, pick, dma, arrive, send, finish
+
+
+def rank_program(g, core, T, topo):
+    rank = T.rank_of(core)
+    if rank is None:
+        return
+    cp, ms, tt, ts, scan, act, mm, iota, pick, dma, arrive, send, finish = make(g, T)
+    ranks = len(T.cores)
+
+    def f(name, w=None, a=0):
+        full = LOC[name][2] if name in LOC else SCRATCH[name][1][1]
+        return (name, a, full if w is None else a + w)
+
+    def sk(k, name="SK"):
+        return (name, 128 * k, 128 * k + 128)
+
+    dma("y", T.f0[:, :], T.fw[:, :], [], [f("f0")])
+    dma("y", T.la0[:, :], T.la[:, :], [], [f("la0")])
+    dma("y", T.z0[:, :], T.zz[:, :], [], [f("z0")])
+    dma("y", T.tI[:, :], T.th[:, :], [], [f("tI")])
+    iota(f("pi"), [[0, 1]], 1)
+    iota(f("gq"), [[1, 8], [0, 16]], 0)
+    iota(f("rq2"), [[0, 16], [1, 16]], 0)
+    iota(f("rq"), [[0, 8], [1, 16]], 0)
+    iota(f("s16"), [[1, 16]], 0)
+    iota(f("j16"), [[256, 16]], 0)
+    ts(f("pi2"), f("pi"), 15, A.bitwise_and)
+    ts(f("pi3"), f("pi"), 4, A.arith_shift_right)
+    cp(f("rp"), f("pi2"))
+    cp(f("gp"), f("pi3"))
+    ts(f("cSf"), f("gq"), f("gp"), A.is_equal)
+    cp(f("cS"), f("cSf"))
+    for k in range(LV):
+        pick(sk(k), f("cS"), [[0, 8], [1, 16]], -k)
+    ms(f("Fw"), 0.0)
+    for k in range(16):
+        act(f("zm", 256, 256 * k), f("rq2"), AF.Identity, 1.0, 0.0)
+    for k in range(8):
+        act(f("zsp", 256, 256 * k), f("rq2"), AF.Identity, 0.0, 0.0)
+    ts(f("fc"), f("f0"), -2048.0, A.add)
+    cp(f("fh"), f("fc"))
+    dma("y", T.Fw[0:128:16, PAD:PAD + W], T.fh[:, :], [f("fh")], [f("Fw")])
+    tt(f("fl"), f("fc"), f("fh"), A.subtract)
+    dma("y", T.Fw[1:128:16, PAD:PAD + W], T.fl[:, :], [f("fl")], [f("Fw")], True)
+    dma("y", T.Bt[:, PAD:PAD + C], T.bk[:, :], [], [f("Bt", C, PAD)])
+    dma("y", T.X[:, PAD:PAD + W], T.x[:, :], [], [f("X", W, PAD)])
+    cp(f("L0"), f("la0"))
+    ms(f("zsp", 2048, 2048), 0.0)
+    ms(("zm", 0, W, LV), 0.0)
+    ts(f("tmp"), f("gq"), f("gp"), A.not_equal, 100.0, A.mult)
+    tt(f("code"), f("tmp"), f("rq"), A.add)
+    ts(f("m0"), f("rp"), 0.0, A.is_equal)
+    ts(f("zc"), f("rp"), 10.0, A.mult, 5.0, A.add)
+    ts(f("zc2"), f("rp"), 4.0, A.mult, 34.0, A.add)
+    ts(f("tmp"), f("code"), 0.0, A.is_equal, f("zc2"), A.mult)
+    ts(f("tmp2"), f("cSf"), f("zc"), A.mult)
+    tt(f("cZ"), f("tmp"), f("tmp2"), A.add)
+    ts(f("cSb"), f("cSf"), f("m0"), A.mult)
+    ts(f("mask"), f("rq2"), f("rp"), A.is_equal)
+    ts(f("dd", 16), f("s16"), f("gp"), A.is_equal)
+    ts(f("s8"), f("s16"), -8.0, A.add)
+    ts(f("dd", 16, 16), f("s8"), f("gp"), A.is_equal)
+    ts(f("cSbn"), f("cSb"), -1.0, A.mult)
+    ts(f("m1"), f("rp"), 1.0, A.is_equal, 0.03125, A.mult)
+    ts(f("cS1"), f("cSf"), f("m1"), A.mult)
+    ts(f("MSK"), f("rq2"), f("rp"), A.is_le, 16384.0, A.mult)
+    ts(f("idn"), f("code"), f("rp"), A.is_equal)
+    cp(f("cI"), f("idn"))
+
+    def late_constants():
+        ts(f("cSr"), f("cSf"), f("rp"), A.mult)
+        for k in range(LV):
+            pick(sk(k, "MK"), f("cSr"), [[0, 8], [1, 16]], -k)
+        ts(f("cI8"), f("idn"), 8192.0, A.mult)
+        ts(f("cSn"), f("cSf"), -1.0, A.mult)
+        ts(f("cS4"), f("cSf"), 4096.0, A.mult)
+        ts(f("cS4n"), f("cSf"), -4096.0, A.mult)
+        ts(f("cSq"), f("cSf"), -256.0, A.mult)
+        ts(f("C4"), f("cSf"), -0.5, A.mult)
+        ts(f("tmp"), f("rq"), f("rp"), A.is_ge)
+        tt(f("tr"), f("tmp"), f("cSf"), A.mult)
+        ts(f("C1"), f("tr"), 131072.0, A.mult)
+        ts(f("C3"), f("tr"), -0.5, A.mult)
+        ts(f("tmp2"), f("idn"), 1.5, A.mult)
+        tt(f("tmp"), f("tmp2"), f("tr"), A.subtract)
+        cp(f("C2"), f("tmp"))
+        ts(f("m15"), f("rp"), 15.0, A.is_equal, 0.5, A.mult)
+        ts(f("tmp2"), f("code"), 15.0, A.is_equal, f("m15"), A.mult)
+        tt(f("C2f"), f("tmp"), f("tmp2"), A.subtract)
+        ts(f("c01"), f("code"), 1.0, A.is_le)
+        ms(f("ones"), 1.0)
+        ts(f("zc3"), f("rp"), 16.0, A.mult)
+        ts(f("J16"), f("j16"), f("zc3"), A.add)
+        ts(f("c613"), f("rp"), 613.0, A.mult, -15.5 / 32, A.add)
+        ts(f("bG"), f("rp"), -1.0, A.mult, 0.5, A.add)
+        tt(f("bY"), f("bG"), f("m15"), A.add)
+        ts(f("bM"), f("rp"), -1.5, A.mult)
+        ts(f("Tn"), f("tI"), -1.0, A.mult, -0.5, A.add)
+        ts(f("Tp"), f("tI"), 0.5, A.add)
+        cp(f("thr"), f("Tn"))
+
+    def keys_t(prods, pb, null=False):
+        for h in range(2):
+            if null:
+                mm(f(pb, 128, 128 * h), f("ones", 128), f("cSq"), True, False)
+            for i, (rows, sel, nsel) in enumerate(prods):
+                mm(f(pb, 128, 128 * h), f(rows, 128, 128 * h), f(sel), i == 0 and not null, i == len(prods) - 1)
+
+    def diff(prods, wt, pb):
+        mm(f(pb, 256, 256), f("cI"), f("MSK"), True, False)
+        for rows, sel, nsel in prods:
+            mm(f(pb, 256, 256), f(nsel), f(rows), False, False)
+        for h in range(2):
+            mm(f(pb, 128, 256 + 128 * h), f(wt, 128, 128 * h), f("cS"), False, h == 1)
+
+    def mylist(wt, pb, a, stop):
+        for h in range(2):
+            mm(f(pb, 16, a), f(wt, 128, 128 * h), f("dd", 16, 16 * h), h == 0, stop and h == 1)
+
+    def lost(em, pb):
+        for r in range(16):
+            mm(f(pb, 16), sk(r), (em, r, K, 16), False, r == 15)
+
+    def eqs(em, pb, null=0.0):
+        ts(f(em), f(pb, 256, 256), null, A.is_equal, -8192.0, A.mult)
+
+    def offs(of, pb, c):
+        ts((of, 0, 31, 2), f(pb, 16), c, A.add, f("rp"), A.max)
+
+    def scatter(tab, of, data):
+        for s in range(15, -1, -1):
+            cp(("@", f(tab), (of, 2 * s, 2 * s + 1)), f(data, 16, 16 * s))
+
+    FW, XW = f("Fw", W, PAD), f("X", W, PAD)
+    pb = [("bu", "cSb", "cSbn")]
+    pw = [("Vw", "cS", "cSn")]
+    ph = [("Vh", "cS", "cSn"), ("mg", "cS4", "cS4n")]
+
+    def pf(c):
+        return 512 * (c % 2) + CL * (c // 2)
+
+    def turn(out, src, c, stop=True):
+        for k in range(LV):
+            mm(out, sk(k), (src, CE * c + k, CE * (c + 1), LV), k == 0, stop and k == LV - 1)
+
+    def step(s, v, L, z, last, dst):
+        c = int(s[2]) if len(s) == 3 and s[2] in "0123" else 0
+        zs, nx = "zs%d" % (v + 1), "%d" % (v + 1)
+        lanes, ents = CL * c, f("z16", CE, CE * c)
+        k = s[:2]
+        if k == "fg":
+            act(f("FG", CE, CE * c), ("@", FW, f(L, CL, lanes)), AF.Copy)
+        elif k == "fh":
+            act(f("FH", CE, CE * c), ("@", FW, f("Bb", CL, lanes)), AF.Copy)
+        elif k == "zb":
+            mm(f("pX", 256), f("cZ"), f(z))
+            ts(f("i1"), f("pX", 256), 255.0, A.add)
+            ts(f("i2"), f("i1"), 1023, A.bitwise_and)
+            cp(f("bu"), f("i2"))
+            keys_t(pb, "pC")
+            cp(("zsp", 0, W, LV), f(z))
+            tt(f("WTb"), f("pC", 256), f("mask"), A.mult)
+            mylist("WTb", "pC", 16, True)
+            cp(f("bl"), f("pC", 16, 16))
+            cp(f("Bb"), ("@", f("Bt", C, PAD), f("bl")))
+            diff(pb, "WTb", "pC")
+            mm(f("pX", 256, 256), f("cS1"), f("bu"))
+        elif k == "sc":
+            for c in range(NCH):
+                scan(f("z16", CE, CE * c), f("zm", CE, CE * c), f("zsp", CE, CE * c), A.mult, A.add)
+        elif k == "eb":
+            eqs("Emb", "pC")
+        elif k == "ob":
+            mylist("WTb", "pC", 0, False)
+            lost("Emb", "pC")
+            offs("ofb", "pC", float(PAD))
+        elif s == "flf":
+            act(f("FLf"), f("FLc"), AF.Identity, 2048.0)
+            if v == 0:
+                late_constants()
+        elif k == "xl":
+            turn(f("pF", CL, pf(c)), "FG", c)
+        elif k == "ul":
+            ts(f("FLu", CL, lanes), f("pF", CL, pf(c)), 2048.0, A.add)
+            cp(f("FLc", CL, lanes), f("pF", CL, pf(c)))
+            tt(f("D", CE, CE * c), ("@", XW, f("FLu", CL, lanes)), ents, A.subtract)
+        elif k == "xg":
+            turn(f("pF", CL, pf(NCH + c)), "FH", c)
+        elif k == "ug":
+            p = f("pF", CL, pf(NCH + c))
+            ts(f("Gu", CL, lanes), p, 2048.0, A.add)
+            tt(f("E", CE, CE * c), ("@", XW, f("Gu", CL, lanes)), ents, A.subtract)
+            tt(f("eq", CL, lanes), p, f("FLc", CL, lanes), A.is_equal)
+            tt(f("pH", CL, lanes), p, f("FLc", CL, lanes), A.max)
+            tt(f("pH", CL, 256 + lanes), p, f("FLc", CL, lanes), A.min)
+        elif k == "da":
+            act(f("DA", CE, CE * c), f("D", CE, CE * c), AF.Abs)
+        elif k == "sd":
+            turn(f("pd", CL, lanes), "DA", c)
+        elif k == "ea":
+            act(f("EA", CE, CE * c), f("E", CE, CE * c), AF.Abs)
+        elif k == "se":
+            turn(f("pe", CL, lanes), "EA", c, False)
+            mm(f("pe", CL, lanes), f("cI8"), f("eq", CL, lanes), False, True)
+        elif k == "df":
+            act(f("fs"), f("pd", 256), AF.Sign, f("thr"))
+            mm(f("pC", 256), f("C1"), f("ones"), True, False)
+            mm(f("pC", 256), f("C1"), f("fs"), False, True)
+            mm(f("pd", 256, 256), f("C2f"), f("fs"))
+            act(f("pd", 256), f("pd", 256, 256), AF.Relu, f("bY"))
+        elif k == "nn":
+            mm(f("pd", 256, 256), f("C4"), f("fs"))
+            act(f("pd", 256, 256), f("pd", 256, 256), AF.Relu, -7.0)
+        elif k == "nw":
+            tt(f("r1"), f("pX", 256, 256), f("FLf"), A.mult)
+            ts(f("r2"), f("r1"), f("c613"), A.add)
+            tt(f("pC", 256, 256), f("pC", 256), f("r2"), A.min)
+            tt(f("sn"), f("pC", 256, 256), f("FLf"), A.add)
+            ts(f("new"), f("sn"), 4095, A.bitwise_and)
+        elif k == "sl":
+            if last:
+                cp(f("ylo"), f("new"))
+                dma("y", T.yl[:, :], T.ylo[:, :], [f("ylo")], [])
+            else:
+                cp(f("Ls" + nx), f("new"))
+                send(f("Ls" + nx), f("L" + nx), topo, core, dst, "aL" + nx, "lL" + nx)
+        elif k == "wv":
+            ts(f("nC"), f("new"), -2048.0, A.add)
+            tt(f("Vw"), f("pd", 256), f("nC"), A.mult)
+        elif k == "wm":
+            keys_t(pw, "pX")
+            tt(f("WTw"), f("pX", 256), f("mask"), A.mult)
+            diff(pw, "WTw", "pX")
+            mylist("WTw", "pX", 0, False)
+        elif k == "we":
+            eqs("Emw", "pX")
+        elif k == "wl":
+            lost("Emw", "pX")
+        elif k == "wo":
+            offs("ofw", "pX", float(2048 + PAD))
+        elif k == "eg":
+            act(f("gs"), f("pe", 256), AF.Sign, f("Tp"), -1.0)
+            mm(f("pS", 256, 256), f("C3"), f("fs"), True, False)
+            mm(f("pS", 256, 256), f("C2"), f("gs"), False, True)
+            act(f("mg"), f("pS", 256, 256), AF.Relu, f("bM"), 1.0, f("Aac"))
+            mm(f("pS", 256), f("C2"), f("gs"))
+            act(f("fg"), f("pS", 256), AF.Relu, f("bG"))
+        elif k == "h1":
+            tt(f("Vh"), f("pH", 256), f("mg"), A.mult)
+        elif k == "hk":
+            keys_t(ph, "pC", True)
+        elif k == "zi":
+            mm(f("pF", 16, 256), f("cI"), f("J16"), True, False)
+            for r in range(16):
+                mm(f("pF", 16, 256), sk(r, "MK"), ("fg", r, K, 16), False, r == 15)
+            mm(f("pF", 256), f("cS"), f("fg"))
+        elif k == "zz":
+            cp(f("idx"), f("pF", 16, 256))
+            ts(f("zh"), ("@", f("E"), f("idx")), 0.5, A.mult, -0.25, A.add)
+            tt(f("pF", 256, 256), f("pF", 256), f("zh"), A.mult)
+            tt(f(zs), f("pF", 256, 256), f(z), A.add)
+            if last:
+                dma("y", T.yz[:, :], T[zs][:, :], [f(zs)], [])
+            else:
+                send(f(zs), f("z" + nx), topo, core, dst, "aZ" + nx, "lZ" + nx)
+        elif k == "h2":
+            tt(f("WTh"), f("pC", 256), f("mask"), A.mult)
+            diff(ph, "WTh", "pC")
+            mylist("WTh", "pC", 0, False)
+        elif k == "h3":
+            eqs("Emh", "pC", -4096.0)
+            lost("Emh", "pC")
+        elif k == "h4":
+            offs("ofh", "pC", float(PAD + 2048))
+        elif k == "l1":
+            tt(f("Vl"), f("pH", 256, 256), f("mg"), A.mult)
+        elif k == "lm":
+            mm(f("pF", 256, 768), f("c01"), f("Vl"))
+            if last:
+                ts(f("lof"), f("pF", 256, 768), 2048.0, A.add)
+            else:
+                act(f("hm"), f("pF", 256, 768), AF.Identity, 0.0, f("m0"))
+        elif k == "l2":
+            tt(f("lod"), f("pF", 256, 768), f("hm"), A.subtract)
+        elif k == "ff":
+            for b in (2 * c, 2 * c + 1):
+                bank = ("pd", "pX")[b % 2]
+                mm(f(bank), f("cS"), f("Fw", 512, PAD + 512 * b))
+                act(f("Ff", 512, PAD + 512 * b), f(bank), AF.Identity, 2048.0)
+        elif k == "fs":
+            if last:
+                scatter("Ff", "ofh", "lof")
+                dma("y", T.yf[:, :], T.Ff[0:128:16, PAD:PAD + W], [f("Ff")], [])
+            else:
+                scatter("Fw", "ofh", "lod")
+        elif k == "bs":
+            scatter("Bt", "ofb", "new")
+            if last:
+                cp(f("ybo"), f("Bt", C, PAD))
+                dma("y", T.yb[:, :], T.ybo[:, :], [f("ybo")], [])
+        elif k == "hv":
+            ts(f("hd"), ("D", 15, W, LV), 0.5, A.mult, -0.25, A.add)
+        elif k == "vv":
+            tt(f("pd", 256, 256), f("pd", 256, 256), f("hd"), A.mult)
+            tt(f("val"), f("pd", 256, 256), f(z), A.add)
+        elif k == "xs":
+            scatter("X", "ofw", "val")
+            if last:
+                dma("s", T.yx[:, :], T.X[:, PAD:PAD + W], [f("X", W, PAD)], [])
+        elif k == "aa":
+            mm(f("pS", 1, 256), f("cSf"), f("Aac"))
+            cp(f("a1"), f("pS", 1, 256))
+            ts(f("a2"), f("a1"), 15, A.bitwise_and)
+            tt(f("thr"), f("Tn"), f("a2"), A.subtract)
+
+    for v in range(VIS):
+        L, z = "L%d" % v, "z%d" % v
+        last = v == VIS - 1
+        dst = T.cores[(rank + 1 + v % (ranks - 1)) % ranks]
+        if v > 0:
+            src = T.cores[(rank - 1 - (v - 1) % (ranks - 1)) % ranks]
+            n = len(topo.engines(src, core))
+            arrive(f(L), "aL%d" % v, n)
+            arrive(f(z), "aZ%d" % v, n)
+        for s in (ORDER_LAST if last else ORDER).split():
+            step(s, v, L, z, last, dst)
+    finish()

@@ -5,20 +5,22 @@ PAD = 16
 NCH = 4
 CL = K // NCH
 CE = CL * LV
+WAKE, CYC, PEC, GAT, SCA, SLACK = 100.0, 1.0, 0.85, 1.56, 3.8, 60.0
 BASE = ("fg0 fg1 fg2 fg3 zb sc eb xl0 ul0 xl1 ul1 fh0 xl2 ul2 ob fh1 xl3 ul3 fh2 fh3 flf xg0 da0 da1 ug0 xg1 ug1 xg2 sd0 da2 ug2 "
         "xg3 sd1 sd2 da3 sd3 df nn ea0 ug3 nw ea1 ea2 ea3 wv wm se0 se1 hv we ")
 ORDER = BASE + "sl bs vv se2 se3 eg h1 hk l1 zi h2 wl lm zz h3 wo xs aa l2 h4 fs"
 ORDER_LAST = BASE + "sl wl vv wo xs se2 se3 eg h1 hk l1 ff0 zi h2 ff1 lm zz h3 ff2 ff3 bs h4 fs"
 
 SCRATCH, LOC = {}, {}
+DT2 = ("bfloat16", "float16", "uint16")
 for _b, _d, _l in (
         ("", "bfloat16", "X 4112 Fw 4112 FG 4096 FH 4096 D 4096 E 4096 DA 4096 EA 4096 z16 4096 zsp 4096 zm 4096 fh 256 fl 256 eq 256 "
          "fs 256 gs 256 fg 256 mg 256 Emb 256 Emw 256 Emh 256 val 256 hm 256 lod 256"),
         ("kb", "bfloat16", "SK 2048 MK 2048 cS 128 cSr 128 cSn 128 cSb 128 cSbn 128 cS1 128 cS4 128 cS4n 128 cSq 128 cI 128 cI8 128 C1 128 "
          "C2 128 C2f 128 C3 128 C4 128 c01 128 cZ 128 MSK 256 dd 32 J16 16 ones 256"),
         ("", "float32", "Ff 4112 Aac 1 fc 256 FLc 256 FLf 256 r1 256 lof 256 ybo 1024 ylo 256"),
-        ("kf", "float32", "cSf 128 mask 256 rq 128 gq 128 code 128 tr 128 idn 128 tmp 128 tmp2 128 rq2 256 s16 16 s8 16 j16 16 rp 1 "
-         "gp 1 m0 1 m1 1 m15 1 zc 1 zc2 1 zc3 1 c613 1 bY 1 bG 1 bM 1 Tn 1 Tp 1 thr 1"),
+        ("kf", "float32", "cSf 128 mask 256 rq 128 gq 128 code 128 tr 128 idn 128 tmp 128 tmp2 128 tmp3 128 tmp4 128 tmp5 128 rq2 256 s16 16 "
+         "s8 16 j16 16 rp 1 gp 1 m0 1 m1 1 m15 1 zc 1 zc2 1 zc3 1 c613 1 bY 1 bG 1 bM 1 Tn 1 Tp 1 thr 1"),
         ("", "int32", "Bt 1040 tI 1 f0 256 la0 256 i1 256 i2 256 r2 256 sn 256 new 256 zh 256 hd 256"),
         ("ki", "int32", "pi 1 pi2 1 pi3 1 a1 1 a2 1"),
         ("", "float16", "bu 256 nC 256 Vw 256 Vh 256 Vl 256 WTb 256 WTw 256 WTh 256"),
@@ -51,9 +53,7 @@ for _v in range(1, VIS):
 
 def make(g, T):
     queues = {"v": g.vector, "s": g.scalar, "t": g.tensor, "g": g, "y": g.sync}
-    n = {"v": 0, "s": 0, "t": 0, "g": 0}
-    clk = {q: {} for q in queues}
-    snap, hist, bank, final = {}, {}, {}, {}
+    ops, hw, hr, bank, marks = [], {}, {}, {}, {}
     nd = [0]
 
     def ap(o):
@@ -74,75 +74,85 @@ def make(g, T):
     def val(o):
         return o if o is None or isinstance(o, (int, float)) else ap(o)
 
-    def wait(q, tok):
-        s, v = tok
-        if clk[q].get(s, 0) >= v:
-            return
-        queues[q].wait_ge(T.sem[s], v)
-        for a, b in snap.get(tok, {}).items():
-            if clk[q].get(a, 0) < b:
-                clk[q][a] = b
-        clk[q][s] = v
+    def rec(q, reads, writes, call, cost, tail=0.0, tok=None, own=True, extra=(), beside=False):
+        i = len(ops)
+        deps = {}
 
-    def banks(o):
-        return range(o[1] // 512, (o[2] - 1) // 512 + 1) if o[0] in PSUM else ()
-
-    def order(q, reads, writes, own):
-        need = {}
-
-        def want(tok):
-            if need.get(tok[0], 0) < tok[1]:
-                need[tok[0]] = tok[1]
+        def dep(j, w):
+            deps[j] = deps.get(j, False) or w
         for o, w in [(r, False) for r in reads] + [(r, True) for r in writes]:
-            for h in hist.get(o[0], []):
-                if h[1] <= o[1] or h[0] >= o[2] or not (w or h[4]):
-                    continue
-                if h[2] == q and own and w and (q == "t" or not h[4]):
-                    continue
-                want(h[3])
-            for b in banks(o):
-                for q2, tok in bank.get((o[0], b), {}).items():
-                    if q2 != q:
-                        want(tok)
-        for s in need:
-            wait(q, (s, need[s]))
+            if w and beside:
+                continue
+            for h in hw.get(o[0], []):
+                if h[0] < o[2] and o[1] < h[1]:
+                    dep(h[2], not (own and ops[h[2]][0] == q and w and q == "t"))
+            if w:
+                for h in hr.get(o[0], []):
+                    if h[0] < o[2] and o[1] < h[1]:
+                        dep(h[2], not (own and ops[h[2]][0] == q))
+        for o in reads + writes:
+            if o[0] in PSUM:
+                for b in range(o[1] // 512, (o[2] - 1) // 512 + 1):
+                    k = bank.setdefault((o[0], b), {})
+                    for q2 in k:
+                        if k[q2] != i:
+                            dep(k[q2], q2 != q)
+                    k[q] = i
+        for j in extra:
+            dep(j, True)
+        ops.append((q, call, deps, cost, tail, tok))
+        for o in reads:
+            hr.setdefault(o[0], []).append((o[1], o[2], i))
+        for o in writes:
+            if (len(o) < 4 or o[3] == 1) and not beside:
+                for h in (hw, hr):
+                    h[o[0]] = [e for e in h.get(o[0], []) if not (o[1] <= e[0] and e[1] <= o[2])]
+            hw.setdefault(o[0], []).append((o[1], o[2], i))
+        return i
 
-    def note(q, reads, writes, tok):
-        snap[tok] = dict(clk.get(q, {}))
-        for o, w in [(r, False) for r in reads] + [(r, True) for r in writes]:
-            h = hist.setdefault(o[0], [])
-            if w and (len(o) < 4 or o[3] == 1):
-                h[:] = [e for e in h if not (o[1] <= e[0] and e[1] <= o[2])]
-            if not w:
-                h[:] = [e for e in h if not (e[2] == q and not e[4] and o[1] <= e[0] and e[1] <= o[2] and e[3][0] == tok[0])]
-            h.append((o[1], o[2], q, tok, w))
-            for b in banks(o):
-                bank.setdefault((o[0], b), {})[q] = tok
-        final[tok[0]] = max(final.get(tok[0], 0), tok[1])
+    def num(o):
+        if o[0] == "@":
+            return LV * num(o[2])
+        return -(-(o[2] - o[1]) // (o[3] if len(o) > 3 else 1))
 
-    def comp(q, reads, writes, call):
-        order(q, reads, writes, True)
-        n[q] += 1
-        call(queues[q]).then_inc(T.sem["q_" + q], 1)
-        note(q, reads, writes, ("q_" + q, n[q]))
+    def two(*l):
+        for o in l:
+            o = o[1] if o[0] == "@" else o
+            if SCRATCH[LOC[o[0]][0] if o[0] in LOC else o[0]][2] not in DT2:
+                return 1.0
+        return 0.5
+
+    def vec(out, ins, call, rate):
+        n = num(out)
+        cost = max(64.0, rate * n) * CYC
+        for o in ins:
+            if not isinstance(o, (int, float)) and o[0] == "@":
+                cost = 50.0 + GAT * n * CYC
+        if out[0] == "@":
+            cost = 50.0 + SCA * n * CYC
+        reads, writes = sum([regs(o) for o in ins], []), regs(out)
+        if out[0] == "@":
+            reads, writes = reads + regs(out[2]), regs(out[1])
+        rec("v", reads, writes, call, cost)
 
     def cp(out, in_):
-        comp("v", regs(in_), regs(out), lambda e: e.tensor_copy(ap(out), ap(in_)))
+        vec(out, [in_], lambda e: e.tensor_copy(ap(out), ap(in_)), two(out, in_))
 
     def ms(out, c):
-        comp("v", [], regs(out), lambda e: e.memset(ap(out), c))
+        vec(out, [], lambda e: e.memset(ap(out), c), two(out))
 
     def tt(out, a, b, op):
-        comp("v", regs(a) + regs(b), regs(out), lambda e: e.tensor_tensor(ap(out), ap(a), ap(b), op))
+        vec(out, [a, b], lambda e: e.tensor_tensor(ap(out), ap(a), ap(b), op), 1.0 if a[0] in PSUM or b[0] in PSUM else 2.0)
 
     def ts(out, a, s1, op0, s2=None, op1=None):
+        ins = [o for o in (a, s1, s2) if o is not None]
         if op1 is None:
-            comp("v", regs(a) + regs(s1), regs(out), lambda e: e.tensor_scalar(ap(out), ap(a), val(s1), None, op0))
+            vec(out, ins, lambda e: e.tensor_scalar(ap(out), ap(a), val(s1), None, op0), two(out, a))
         else:
-            comp("v", regs(a) + regs(s1) + regs(s2), regs(out), lambda e: e.tensor_scalar(ap(out), ap(a), val(s1), val(s2), op0, op1))
+            vec(out, ins, lambda e: e.tensor_scalar(ap(out), ap(a), val(s1), val(s2), op0, op1), two(out, a))
 
     def scan(out, a, b, op0, op1):
-        comp("v", regs(a) + regs(b), regs(out), lambda e: e.tensor_tensor_scan(ap(out), ap(a), ap(b), 0.0, op0, op1))
+        vec(out, [a, b], lambda e: e.tensor_tensor_scan(ap(out), ap(a), ap(b), 0.0, op0, op1), two(out, a, b))
 
     def act(out, in_, func, bias=0.0, scale=1.0, acc=None):
         kw = {}
@@ -152,45 +162,120 @@ def make(g, T):
             kw["bias"] = val(bias)
         if not (isinstance(scale, float) and scale == 1.0):
             kw["scale"] = val(scale)
-        comp("s", regs(in_) + regs(bias) + regs(scale), regs(out) + regs(acc), lambda e: e.activation(ap(out), ap(in_), func, **kw))
+        n = num(out)
+        cost = 65.0 + GAT * n * CYC if in_[0] == "@" else max(64.0, n) * CYC
+        rec("s", regs(in_) + regs(bias) + regs(scale), regs(out) + regs(acc), lambda e: e.activation(ap(out), ap(in_), func, **kw), cost)
 
     def mm(out, lhsT, rhs, start=True, stop=True):
-        comp("t", regs(lhsT) + regs(rhs), regs(out), lambda e: e.matmul(ap(out), ap(lhsT), ap(rhs), start, stop))
+        rec("t", regs(lhsT) + regs(rhs), regs(out), lambda e: e.matmul(ap(out), ap(lhsT), ap(rhs), start, stop), max(64.0, num(out)) * PEC)
 
     def iota(out, pattern, mult):
-        comp("g", [], regs(out), lambda e: e.iota(ap(out), pattern, 0, mult, allow_small_or_imprecise_dtypes=True))
+        rec("g", [], regs(out), lambda e: e.iota(ap(out), pattern, 0, mult, allow_small_or_imprecise_dtypes=True), 130.0 + 2 * num(out))
 
     def pick(out, in_, pattern, base):
-        comp("g", regs(in_), regs(out), lambda e: e.affine_select(ap(out), ap(in_), pattern, A.is_equal, 0.0, base, 0))
+        rec("g", regs(in_), regs(out), lambda e: e.affine_select(ap(out), ap(in_), pattern, A.is_equal, 0.0, base, 0), 170.0 + 2 * num(out))
 
-    def dma(q, out, in_, reads, writes, beside=False):
-        order(q, reads, [] if beside else writes, False)
+    def dma(q, out, in_, reads, writes, beside=False, us=2.5):
         s = "d%d" % nd[0]
         nd[0] += 1
-        queues[q].dma_start(out, in_).then_inc(T.sem[s], 16)
-        note("dma", reads, [o + (2,) for o in writes] if beside else writes, (s, 16))
-        snap[(s, 16)] = dict(clk[q])
+        rec(q, reads, writes, lambda e: e.dma_start(out, in_), 70.0, 1000.0 * us, (s, 16), False, (), beside)
 
-    def arrive(o, s, v):
-        note("in", [], [o], (s, v))
+    def arrive(o, s, v, mark):
+        rec(None, [], [o], None, 0.0, 0.0, (s, v), False, (marks[mark],))
 
-    def send(o, out, topo, core, dst, rs, ls):
-        order("g", regs(o), [], False)
+    def send(o, out, topo, core, dst, rs, ls, mark):
         rid, pid = topo.addr(dst)[0:2]
-        g.remote_dma(ap(out), ap(o), T.sem[rs], T.sem[ls], pid, rid, topo.mask(core, dst))
-        note("out", regs(o), [], (ls, len(topo.engines(core, dst))))
+        marks[mark] = rec("g", regs(o), [], lambda e: e.remote_dma(ap(out), ap(o), T.sem[rs], T.sem[ls], pid, rid, topo.mask(core, dst)),
+                          700.0, 3000.0, (ls, len(topo.engines(core, dst))), False)
 
-    def finish():
+    def issue():
+        n = len(ops)
+        succ, left = [[] for _ in ops], [len(op[2]) for op in ops]
+        for i, op in enumerate(ops):
+            for j in op[2]:
+                succ[j].append(i)
+        prio = [0.0] * n
+        for i in range(n - 1, -1, -1):
+            prio[i] = ops[i][3] + ops[i][4] + max([prio[j] + (WAKE if ops[j][2][i] else 0.0) for j in succ[i]] or [0.0])
+        free = {q: 0.0 for q in queues}
+        done, start = [0.0] * n, [0.0] * n
+        ready = {q: [] for q in queues}
+        seq = []
+
+        def put(i):
+            t = max([done[j] if ops[i][2][j] else start[j] for j in ops[i][2]] or [-1.0])
+            if ops[i][0] is None:
+                finish(i, t)
+            else:
+                ready[ops[i][0]].append((t, i))
+
+        def finish(i, t):
+            start[i], done[i] = t, t + ops[i][3] + ops[i][4]
+            seq.append(i)
+            for j in succ[i]:
+                left[j] -= 1
+                if left[j] == 0:
+                    put(j)
+        for i in range(n):
+            if not ops[i][2]:
+                put(i)
+        while len(seq) < n:
+            best = None
+            for q in queues:
+                if not ready[q]:
+                    continue
+                c = [((free[q] if t < free[q] else t + WAKE), i) for t, i in ready[q]]
+                m = min(c)[0]
+                s, i = max([(prio[i], s, i) for s, i in c if s <= m + SLACK])[1:]
+                if best is None or s < best[0]:
+                    best = (s, q, i)
+            s, q, i = best
+            ready[q] = [e for e in ready[q] if e[1] != i]
+            free[q] = s + ops[i][3]
+            finish(i, s)
+        clk, snap, final = {q: {} for q in queues}, {}, {}
+        cnt, token = {"v": 0, "s": 0, "t": 0, "g": 0}, {}
+
+        def wait(q, tok):
+            s, v = tok
+            if clk[q].get(s, 0) >= v:
+                return
+            queues[q].wait_ge(T.sem[s], v)
+            for a in snap[tok]:
+                if clk[q].get(a, 0) < snap[tok][a]:
+                    clk[q][a] = snap[tok][a]
+            clk[q][s] = v
+        for i in seq:
+            q, call, deps, cost, tail, tok = ops[i]
+            need = {}
+            for j in deps:
+                if deps[j] and q is not None:
+                    need[token[j][0]] = max(need.get(token[j][0], 0), token[j][1])
+            for s in need:
+                wait(q, (s, need[s]))
+            if q is None:
+                snap[tok] = {}
+            else:
+                ins = call(queues[q])
+                if tok is None:
+                    cnt[q] += 1
+                    tok = ("q_" + q, cnt[q])
+                    ins.then_inc(T.sem[tok[0]], 1)
+                elif tok[0][0] == "d":
+                    ins.then_inc(T.sem[tok[0]], 16)
+                snap[tok] = dict(clk[q])
+            token[i] = tok
+            final[tok[0]] = max(final.get(tok[0], 0), tok[1])
         for s in final:
             wait("g", (s, final[s]))
-    return cp, ms, tt, ts, scan, act, mm, iota, pick, dma, arrive, send, finish
+    return cp, ms, tt, ts, scan, act, mm, iota, pick, dma, arrive, send, issue
 
 
 def rank_program(g, core, T, topo):
     rank = T.rank_of(core)
     if rank is None:
         return
-    cp, ms, tt, ts, scan, act, mm, iota, pick, dma, arrive, send, finish = make(g, T)
+    cp, ms, tt, ts, scan, act, mm, iota, pick, dma, arrive, send, issue = make(g, T)
     ranks = len(T.cores)
 
     def f(name, w=None, a=0):
@@ -228,8 +313,8 @@ def rank_program(g, core, T, topo):
     dma("y", T.Fw[0:128:16, PAD:PAD + W], T.fh[:, :], [f("fh")], [f("Fw")])
     tt(f("fl"), f("fc"), f("fh"), A.subtract)
     dma("y", T.Fw[1:128:16, PAD:PAD + W], T.fl[:, :], [f("fl")], [f("Fw")], True)
-    dma("y", T.Bt[:, PAD:PAD + C], T.bk[:, :], [], [f("Bt", C, PAD)])
-    dma("y", T.X[:, PAD:PAD + W], T.x[:, :], [], [f("X", W, PAD)])
+    dma("y", T.Bt[:, PAD:PAD + C], T.bk[:, :], [], [f("Bt", C, PAD)], False, 4.0)
+    dma("y", T.X[:, PAD:PAD + W], T.x[:, :], [], [f("X", W, PAD)], False, 7.0)
     cp(f("L0"), f("la0"))
     ms(f("zsp", 2048, 2048), 0.0)
     ms(("zm", 0, W, LV), 0.0)
@@ -238,9 +323,9 @@ def rank_program(g, core, T, topo):
     ts(f("m0"), f("rp"), 0.0, A.is_equal)
     ts(f("zc"), f("rp"), 10.0, A.mult, 5.0, A.add)
     ts(f("zc2"), f("rp"), 4.0, A.mult, 34.0, A.add)
-    ts(f("tmp"), f("code"), 0.0, A.is_equal, f("zc2"), A.mult)
+    ts(f("tmp4"), f("code"), 0.0, A.is_equal, f("zc2"), A.mult)
     ts(f("tmp2"), f("cSf"), f("zc"), A.mult)
-    tt(f("cZ"), f("tmp"), f("tmp2"), A.add)
+    tt(f("cZ"), f("tmp4"), f("tmp2"), A.add)
     ts(f("cSb"), f("cSf"), f("m0"), A.mult)
     ts(f("mask"), f("rq2"), f("rp"), A.is_equal)
     ts(f("dd", 16), f("s16"), f("gp"), A.is_equal)
@@ -263,16 +348,16 @@ def rank_program(g, core, T, topo):
         ts(f("cS4n"), f("cSf"), -4096.0, A.mult)
         ts(f("cSq"), f("cSf"), -256.0, A.mult)
         ts(f("C4"), f("cSf"), -0.5, A.mult)
-        ts(f("tmp"), f("rq"), f("rp"), A.is_ge)
-        tt(f("tr"), f("tmp"), f("cSf"), A.mult)
+        ts(f("tmp3"), f("rq"), f("rp"), A.is_ge)
+        tt(f("tr"), f("tmp3"), f("cSf"), A.mult)
         ts(f("C1"), f("tr"), 131072.0, A.mult)
         ts(f("C3"), f("tr"), -0.5, A.mult)
         ts(f("tmp2"), f("idn"), 1.5, A.mult)
         tt(f("tmp"), f("tmp2"), f("tr"), A.subtract)
         cp(f("C2"), f("tmp"))
         ts(f("m15"), f("rp"), 15.0, A.is_equal, 0.5, A.mult)
-        ts(f("tmp2"), f("code"), 15.0, A.is_equal, f("m15"), A.mult)
-        tt(f("C2f"), f("tmp"), f("tmp2"), A.subtract)
+        ts(f("tmp5"), f("code"), 15.0, A.is_equal, f("m15"), A.mult)
+        tt(f("C2f"), f("tmp"), f("tmp5"), A.subtract)
         ts(f("c01"), f("code"), 1.0, A.is_le)
         ms(f("ones"), 1.0)
         ts(f("zc3"), f("rp"), 16.0, A.mult)
@@ -375,10 +460,10 @@ def rank_program(g, core, T, topo):
         elif k == "ug":
             p = f("pF", CL, pf(NCH + c))
             ts(f("Gu", CL, lanes), p, 2048.0, A.add)
-            tt(f("E", CE, CE * c), ("@", XW, f("Gu", CL, lanes)), ents, A.subtract)
             tt(f("eq", CL, lanes), p, f("FLc", CL, lanes), A.is_equal)
             tt(f("pH", CL, lanes), p, f("FLc", CL, lanes), A.max)
             tt(f("pH", CL, 256 + lanes), p, f("FLc", CL, lanes), A.min)
+            tt(f("E", CE, CE * c), ("@", XW, f("Gu", CL, lanes)), ents, A.subtract)
         elif k == "da":
             act(f("DA", CE, CE * c), f("D", CE, CE * c), AF.Abs)
         elif k == "sd":
@@ -409,7 +494,7 @@ def rank_program(g, core, T, topo):
                 dma("y", T.yl[:, :], T.ylo[:, :], [f("ylo")], [])
             else:
                 cp(f("Ls" + nx), f("new"))
-                send(f("Ls" + nx), f("L" + nx), topo, core, dst, "aL" + nx, "lL" + nx)
+                send(f("Ls" + nx), f("L" + nx), topo, core, dst, "aL" + nx, "lL" + nx, "L" + nx)
         elif k == "wv":
             ts(f("nC"), f("new"), -2048.0, A.add)
             tt(f("Vw"), f("pd", 256), f("nC"), A.mult)
@@ -448,7 +533,7 @@ def rank_program(g, core, T, topo):
             if last:
                 dma("y", T.yz[:, :], T[zs][:, :], [f(zs)], [])
             else:
-                send(f(zs), f("z" + nx), topo, core, dst, "aZ" + nx, "lZ" + nx)
+                send(f(zs), f("z" + nx), topo, core, dst, "aZ" + nx, "lZ" + nx, "Z" + nx)
         elif k == "h2":
             tt(f("WTh"), f("pC", 256), f("mask"), A.mult)
             diff(ph, "WTh", "pC")
@@ -483,7 +568,7 @@ def rank_program(g, core, T, topo):
             scatter("Bt", "ofb", "new")
             if last:
                 cp(f("ybo"), f("Bt", C, PAD))
-                dma("y", T.yb[:, :], T.ybo[:, :], [f("ybo")], [])
+                dma("y", T.yb[:, :], T.ybo[:, :], [f("ybo")], [], False, 4.5)
         elif k == "hv":
             ts(f("hd"), ("D", 15, W, LV), 0.5, A.mult, -0.25, A.add)
         elif k == "vv":
@@ -492,7 +577,7 @@ def rank_program(g, core, T, topo):
         elif k == "xs":
             scatter("X", "ofw", "val")
             if last:
-                dma("s", T.yx[:, :], T.X[:, PAD:PAD + W], [f("X", W, PAD)], [])
+                dma("s", T.yx[:, :], T.X[:, PAD:PAD + W], [f("X", W, PAD)], [], False, 7.0)
         elif k == "aa":
             mm(f("pS", 1, 256), f("cSf"), f("Aac"))
             cp(f("a1"), f("pS", 1, 256))
@@ -506,8 +591,8 @@ def rank_program(g, core, T, topo):
         if v > 0:
             src = T.cores[(rank - 1 - (v - 1) % (ranks - 1)) % ranks]
             n = len(topo.engines(src, core))
-            arrive(f(L), "aL%d" % v, n)
-            arrive(f(z), "aZ%d" % v, n)
+            arrive(f(L), "aL%d" % v, n, "L%d" % v)
+            arrive(f(z), "aZ%d" % v, n, "Z%d" % v)
         for s in (ORDER_LAST if last else ORDER).split():
             step(s, v, L, z, last, dst)
-    finish()
+    issue()

from concourse.mybir import AluOpType as A, ActivationFunctionType as AF

VIS, W, C, K, LV = 5, 4096, 1024, 256, 16
PAD = 16
NCH = 4
CL = K // NCH
CE = CL * LV
WAKE, CYC, PEC, GAT, SCA, SLACK = 100.0, 1.0, 0.85, 1.56, 3.8, 60.0
BASE = ("fg0 fg1 fg2 fg3 zb sc eb xl0 ul0 xl1 ul1 fh0 xl2 ul2 ob fh1 xl3 ul3 fh2 fh3 flf xg0 da0 da1 ug0 xg1 ug1 xg2 sd0 da2 ug2 "
        "xg3 sd1 sd2 da3 sd3 df nn ea0 ug3 nw ea1 ea2 ea3 wv wm se0 se1 hv we ")
ORDER = BASE + "sl bs vv se2 se3 eg h1 hk l1 zi h2 wl lm zz h3 wo xs aa l2 h4 fs"
ORDER_LAST = BASE + "sl wl vv wo xs se2 se3 eg h1 hk l1 ff0 zi h2 ff1 lm zz h3 ff2 ff3 bs h4 fs"

SCRATCH, LOC = {}, {}
DT2 = ("bfloat16", "float16", "uint16")
for _b, _d, _l in (
        ("", "bfloat16", "X 4112 Fw 4112 FG 4096 FH 4096 D 4096 E 4096 DA 4096 EA 4096 z16 4096 zsp 4096 zm 4096 fh 256 fl 256 eq 256 "
         "fs 256 gs 256 fg 256 mg 256 Emb 256 Emw 256 Emh 256 val 256 hm 256 lod 256"),
        ("kb", "bfloat16", "SK 2048 MK 2048 cS 128 cSr 128 cSn 128 cSb 128 cSbn 128 cS1 128 cS4 128 cS4n 128 cSq 128 cI 128 cI8 128 C1 128 "
         "C2 128 C2f 128 C3 128 C4 128 c01 128 cZ 128 MSK 256 dd 32 J16 16 ones 256"),
        ("", "float32", "Ff 4112 Aac 1 fc 256 FLc 256 FLf 256 r1 256 lof 256 ybo 1024 ylo 256"),
        ("kf", "float32", "cSf 128 mask 256 rq 128 gq 128 code 128 tr 128 idn 128 tmp 128 tmp2 128 tmp3 128 tmp4 128 tmp5 128 rq2 256 s16 16 "
         "s8 16 j16 16 rp 1 gp 1 m0 1 m1 1 m15 1 zc 1 zc2 1 zc3 1 c613 1 bY 1 bG 1 bM 1 Tn 1 Tp 1 thr 1"),
        ("", "int32", "Bt 1040 tI 1 f0 256 la0 256 i1 256 i2 256 r2 256 sn 256 new 256 zh 256 hd 256"),
        ("ki", "int32", "pi 1 pi2 1 pi3 1 a1 1 a2 1"),
        ("", "float16", "bu 256 nC 256 Vw 256 Vh 256 Vl 256 WTb 256 WTw 256 WTh 256"),
        ("", "uint16", "bl 16 Bb 256 FLu 256 Gu 256 ofb 32 ofw 32 ofh 32 idx 16")):
    _l, _c = _l.split(), 0
    for _i in range(0, len(_l), 2):
        _n, _w = _l[_i], int(_l[_i + 1])
        if _b:
            LOC[_n] = (_b, _c, _w)
            _c += (_w + 15) // 16 * 16
            SCRATCH[_b] = ("sbuf", [128, _c], _d)
        else:
            SCRATCH[_n] = ("sbuf", [128, _w], _d)
for _v in range(VIS + 1):
    if _v < VIS:
        SCRATCH["L%d" % _v] = ("sbuf", [128, K], "uint16")
        SCRATCH["z%d" % _v] = ("sbuf", [128, K], "bfloat16")
    if _v > 0:
        SCRATCH["zs%d" % _v] = ("sbuf", [128, K], "bfloat16")
    if 0 < _v < VIS:
        SCRATCH["Ls%d" % _v] = ("sbuf", [128, K], "uint16")
PSUM = {"pF": 1024, "pd": 512, "pe": 512, "pC": 512, "pS": 512, "pH": 512, "pX": 512}
for _n in PSUM:
    SCRATCH[_n] = ("psum", [128, PSUM[_n]], "float32")
NDMA = 16
SEMAPHORES = ["q_v", "q_s", "q_t", "q_g"] + ["d%d" % i for i in range(NDMA)]
for _v in range(1, VIS):
    SEMAPHORES += ["aL%d" % _v, "aZ%d" % _v, "lL%d" % _v, "lZ%d" % _v]


def make(g, T):
    queues = {"v": g.vector, "s": g.scalar, "t": g.tensor, "g": g, "y": g.sync}
    ops, hw, hr, bank, marks = [], {}, {}, {}, {}
    nd = [0]

    def ap(o):
        if o[0] == "@":
            return ap(o[1]).indirect(ap(o[2]))
        b, a = (LOC[o[0]][0], LOC[o[0]][1]) if o[0] in LOC else (o[0], 0)
        if len(o) == 4 and o[3] != 1:
            return T[b][:, a + o[1]:a + o[2]:o[3]]
        return T[b][:, a + o[1]:a + o[2]]

    def regs(o):
        if o is None or isinstance(o, (int, float)):
            return []
        if o[0] == "@":
            return regs(o[1]) + regs(o[2])
        return [o]

    def val(o):
        return o if o is None or isinstance(o, (int, float)) else ap(o)

    def rec(q, reads, writes, call, cost, tail=0.0, tok=None, own=True, extra=(), beside=False):
        i = len(ops)
        deps = {}

        def dep(j, w):
            deps[j] = deps.get(j, False) or w
        for o, w in [(r, False) for r in reads] + [(r, True) for r in writes]:
            if w and beside:
                continue
            for h in hw.get(o[0], []):
                if h[0] < o[2] and o[1] < h[1]:
                    dep(h[2], not (own and ops[h[2]][0] == q and w and q == "t"))
            if w:
                for h in hr.get(o[0], []):
                    if h[0] < o[2] and o[1] < h[1]:
                        dep(h[2], not (own and ops[h[2]][0] == q))
        for o in reads + writes:
            if o[0] in PSUM:
                for b in range(o[1] // 512, (o[2] - 1) // 512 + 1):
                    k = bank.setdefault((o[0], b), {})
                    for q2 in k:
                        if k[q2] != i:
                            dep(k[q2], q2 != q)
                    k[q] = i
        for j in extra:
            dep(j, True)
        ops.append((q, call, deps, cost, tail, tok))
        for o in reads:
            hr.setdefault(o[0], []).append((o[1], o[2], i))
        for o in writes:
            if (len(o) < 4 or o[3] == 1) and not beside:
                for h in (hw, hr):
                    h[o[0]] = [e for e in h.get(o[0], []) if not (o[1] <= e[0] and e[1] <= o[2])]
            hw.setdefault(o[0], []).append((o[1], o[2], i))
        return i

    def num(o):
        if o[0] == "@":
            return LV * num(o[2])
        return -(-(o[2] - o[1]) // (o[3] if len(o) > 3 else 1))

    def two(*l):
        for o in l:
            o = o[1] if o[0] == "@" else o
            if SCRATCH[LOC[o[0]][0] if o[0] in LOC else o[0]][2] not in DT2:
                return 1.0
        return 0.5

    def vec(out, ins, call, rate):
        n = num(out)
        cost = max(64.0, rate * n) * CYC
        for o in ins:
            if not isinstance(o, (int, float)) and o[0] == "@":
                cost = 50.0 + GAT * n * CYC
        if out[0] == "@":
            cost = 50.0 + SCA * n * CYC
        reads, writes = sum([regs(o) for o in ins], []), regs(out)
        if out[0] == "@":
            reads, writes = reads + regs(out[2]), regs(out[1])
        rec("v", reads, writes, call, cost)

    def cp(out, in_):
        vec(out, [in_], lambda e: e.tensor_copy(ap(out), ap(in_)), two(out, in_))

    def ms(out, c):
        vec(out, [], lambda e: e.memset(ap(out), c), two(out))

    def tt(out, a, b, op):
        vec(out, [a, b], lambda e: e.tensor_tensor(ap(out), ap(a), ap(b), op), 1.0 if a[0] in PSUM or b[0] in PSUM else 2.0)

    def ts(out, a, s1, op0, s2=None, op1=None):
        ins = [o for o in (a, s1, s2) if o is not None]
        if op1 is None:
            vec(out, ins, lambda e: e.tensor_scalar(ap(out), ap(a), val(s1), None, op0), two(out, a))
        else:
            vec(out, ins, lambda e: e.tensor_scalar(ap(out), ap(a), val(s1), val(s2), op0, op1), two(out, a))

    def scan(out, a, b, op0, op1):
        vec(out, [a, b], lambda e: e.tensor_tensor_scan(ap(out), ap(a), ap(b), 0.0, op0, op1), two(out, a, b))

    def act(out, in_, func, bias=0.0, scale=1.0, acc=None):
        kw = {}
        if acc is not None:
            kw["accum_out"] = ap(acc)
        if not (isinstance(bias, float) and bias == 0.0):
            kw["bias"] = val(bias)
        if not (isinstance(scale, float) and scale == 1.0):
            kw["scale"] = val(scale)
        n = num(out)
        cost = 65.0 + GAT * n * CYC if in_[0] == "@" else max(64.0, n) * CYC
        rec("s", regs(in_) + regs(bias) + regs(scale), regs(out) + regs(acc), lambda e: e.activation(ap(out), ap(in_), func, **kw), cost)

    def mm(out, lhsT, rhs, start=True, stop=True):
        rec("t", regs(lhsT) + regs(rhs), regs(out), lambda e: e.matmul(ap(out), ap(lhsT), ap(rhs), start, stop), max(64.0, num(out)) * PEC)

    def iota(out, pattern, mult):
        rec("g", [], regs(out), lambda e: e.iota(ap(out), pattern, 0, mult, allow_small_or_imprecise_dtypes=True), 130.0 + 2 * num(out))

    def pick(out, in_, pattern, base):
        rec("g", regs(in_), regs(out), lambda e: e.affine_select(ap(out), ap(in_), pattern, A.is_equal, 0.0, base, 0), 170.0 + 2 * num(out))

    def dma(q, out, in_, reads, writes, beside=False, us=2.5):
        s = "d%d" % nd[0]
        nd[0] += 1
        rec(q, reads, writes, lambda e: e.dma_start(out, in_), 70.0, 1000.0 * us, (s, 16), False, (), beside)

    def arrive(o, s, v, mark):
        rec(None, [], [o], None, 0.0, 0.0, (s, v), False, (marks[mark],))

    def send(o, out, topo, core, dst, rs, ls, mark):
        rid, pid = topo.addr(dst)[0:2]
        marks[mark] = rec("g", regs(o), [], lambda e: e.remote_dma(ap(out), ap(o), T.sem[rs], T.sem[ls], pid, rid, topo.mask(core, dst)),
                          700.0, 3000.0, (ls, len(topo.engines(core, dst))), False)

    def issue():
        n = len(ops)
        succ, left = [[] for _ in ops], [len(op[2]) for op in ops]
        for i, op in enumerate(ops):
            for j in op[2]:
                succ[j].append(i)
        prio = [0.0] * n
        for i in range(n - 1, -1, -1):
            prio[i] = ops[i][3] + ops[i][4] + max([prio[j] + (WAKE if ops[j][2][i] else 0.0) for j in succ[i]] or [0.0])
        free = {q: 0.0 for q in queues}
        done, start = [0.0] * n, [0.0] * n
        ready = {q: [] for q in queues}
        seq = []

        def put(i):
            t = max([done[j] if ops[i][2][j] else start[j] for j in ops[i][2]] or [-1.0])
            if ops[i][0] is None:
                finish(i, t)
            else:
                ready[ops[i][0]].append((t, i))

        def finish(i, t):
            start[i], done[i] = t, t + ops[i][3] + ops[i][4]
            seq.append(i)
            for j in succ[i]:
                left[j] -= 1
                if left[j] == 0:
                    put(j)
        for i in range(n):
            if not ops[i][2]:
                put(i)
        while len(seq) < n:
            best = None
            for q in queues:
                if not ready[q]:
                    continue
                c = [((free[q] if t < free[q] else t + WAKE), i) for t, i in ready[q]]
                m = min(c)[0]
                s, i = max([(prio[i], s, i) for s, i in c if s <= m + SLACK])[1:]
                if best is None or s < best[0]:
                    best = (s, q, i)
            s, q, i = best
            ready[q] = [e for e in ready[q] if e[1] != i]
            free[q] = s + ops[i][3]
            finish(i, s)
        clk, snap, final = {q: {} for q in queues}, {}, {}
        cnt, token = {"v": 0, "s": 0, "t": 0, "g": 0}, {}

        def wait(q, tok):
            s, v = tok
            if clk[q].get(s, 0) >= v:
                return
            queues[q].wait_ge(T.sem[s], v)
            for a in snap[tok]:
                if clk[q].get(a, 0) < snap[tok][a]:
                    clk[q][a] = snap[tok][a]
            clk[q][s] = v
        for i in seq:
            q, call, deps, cost, tail, tok = ops[i]
            need = {}
            for j in deps:
                if deps[j] and q is not None:
                    need[token[j][0]] = max(need.get(token[j][0], 0), token[j][1])
            for s in need:
                wait(q, (s, need[s]))
            if q is None:
                snap[tok] = {}
            else:
                ins = call(queues[q])
                if tok is None:
                    cnt[q] += 1
                    tok = ("q_" + q, cnt[q])
                    ins.then_inc(T.sem[tok[0]], 1)
                elif tok[0][0] == "d":
                    ins.then_inc(T.sem[tok[0]], 16)
                snap[tok] = dict(clk[q])
            token[i] = tok
            final[tok[0]] = max(final.get(tok[0], 0), tok[1])
        for s in final:
            wait("g", (s, final[s]))
    return cp, ms, tt, ts, scan, act, mm, iota, pick, dma, arrive, send, issue


def rank_program(g, core, T, topo):
    rank = T.rank_of(core)
    if rank is None:
        return
    cp, ms, tt, ts, scan, act, mm, iota, pick, dma, arrive, send, issue = make(g, T)
    ranks = len(T.cores)

    def f(name, w=None, a=0):
        full = LOC[name][2] if name in LOC else SCRATCH[name][1][1]
        return (name, a, full if w is None else a + w)

    def sk(k, name="SK"):
        return (name, 128 * k, 128 * k + 128)

    dma("y", T.f0[:, :], T.fw[:, :], [], [f("f0")])
    dma("y", T.la0[:, :], T.la[:, :], [], [f("la0")])
    dma("y", T.z0[:, :], T.zz[:, :], [], [f("z0")])
    dma("y", T.tI[:, :], T.th[:, :], [], [f("tI")])
    iota(f("pi"), [[0, 1]], 1)
    iota(f("gq"), [[1, 8], [0, 16]], 0)
    iota(f("rq2"), [[0, 16], [1, 16]], 0)
    iota(f("rq"), [[0, 8], [1, 16]], 0)
    iota(f("s16"), [[1, 16]], 0)
    iota(f("j16"), [[256, 16]], 0)
    ts(f("pi2"), f("pi"), 15, A.bitwise_and)
    ts(f("pi3"), f("pi"), 4, A.arith_shift_right)
    cp(f("rp"), f("pi2"))
    cp(f("gp"), f("pi3"))
    ts(f("cSf"), f("gq"), f("gp"), A.is_equal)
    cp(f("cS"), f("cSf"))
    for k in range(LV):
        pick(sk(k), f("cS"), [[0, 8], [1, 16]], -k)
    ms(f("Fw"), 0.0)
    for k in range(16):
        act(f("zm", 256, 256 * k), f("rq2"), AF.Identity, 1.0, 0.0)
    for k in range(8):
        act(f("zsp", 256, 256 * k), f("rq2"), AF.Identity, 0.0, 0.0)
    ts(f("fc"), f("f0"), -2048.0, A.add)
    cp(f("fh"), f("fc"))
    dma("y", T.Fw[0:128:16, PAD:PAD + W], T.fh[:, :], [f("fh")], [f("Fw")])
    tt(f("fl"), f("fc"), f("fh"), A.subtract)
    dma("y", T.Fw[1:128:16, PAD:PAD + W], T.fl[:, :], [f("fl")], [f("Fw")], True)
    dma("y", T.Bt[:, PAD:PAD + C], T.bk[:, :], [], [f("Bt", C, PAD)], False, 4.0)
    dma("y", T.X[:, PAD:PAD + W], T.x[:, :], [], [f("X", W, PAD)], False, 7.0)
    cp(f("L0"), f("la0"))
    ms(f("zsp", 2048, 2048), 0.0)
    ms(("zm", 0, W, LV), 0.0)
    ts(f("tmp"), f("gq"), f("gp"), A.not_equal, 100.0, A.mult)
    tt(f("code"), f("tmp"), f("rq"), A.add)
    ts(f("m0"), f("rp"), 0.0, A.is_equal)
    ts(f("zc"), f("rp"), 10.0, A.mult, 5.0, A.add)
    ts(f("zc2"), f("rp"), 4.0, A.mult, 34.0, A.add)
    ts(f("tmp4"), f("code"), 0.0, A.is_equal, f("zc2"), A.mult)
    ts(f("tmp2"), f("cSf"), f("zc"), A.mult)
    tt(f("cZ"), f("tmp4"), f("tmp2"), A.add)
    ts(f("cSb"), f("cSf"), f("m0"), A.mult)
    ts(f("mask"), f("rq2"), f("rp"), A.is_equal)
    ts(f("dd", 16), f("s16"), f("gp"), A.is_equal)
    ts(f("s8"), f("s16"), -8.0, A.add)
    ts(f("dd", 16, 16), f("s8"), f("gp"), A.is_equal)
    ts(f("cSbn"), f("cSb"), -1.0, A.mult)
    ts(f("m1"), f("rp"), 1.0, A.is_equal, 0.03125, A.mult)
    ts(f("cS1"), f("cSf"), f("m1"), A.mult)
    ts(f("MSK"), f("rq2"), f("rp"), A.is_le, 16384.0, A.mult)
    ts(f("idn"), f("code"), f("rp"), A.is_equal)
    cp(f("cI"), f("idn"))

    def late_constants():
        ts(f("cSr"), f("cSf"), f("rp"), A.mult)
        for k in range(LV):
            pick(sk(k, "MK"), f("cSr"), [[0, 8], [1, 16]], -k)
        ts(f("cI8"), f("idn"), 8192.0, A.mult)
        ts(f("cSn"), f("cSf"), -1.0, A.mult)
        ts(f("cS4"), f("cSf"), 4096.0, A.mult)
        ts(f("cS4n"), f("cSf"), -4096.0, A.mult)
        ts(f("cSq"), f("cSf"), -256.0, A.mult)
        ts(f("C4"), f("cSf"), -0.5, A.mult)
        ts(f("tmp3"), f("rq"), f("rp"), A.is_ge)
        tt(f("tr"), f("tmp3"), f("cSf"), A.mult)
        ts(f("C1"), f("tr"), 131072.0, A.mult)
        ts(f("C3"), f("tr"), -0.5, A.mult)
        ts(f("tmp2"), f("idn"), 1.5, A.mult)
        tt(f("tmp"), f("tmp2"), f("tr"), A.subtract)
        cp(f("C2"), f("tmp"))
        ts(f("m15"), f("rp"), 15.0, A.is_equal, 0.5, A.mult)
        ts(f("tmp5"), f("code"), 15.0, A.is_equal, f("m15"), A.mult)
        tt(f("C2f"), f("tmp"), f("tmp5"), A.subtract)
        ts(f("c01"), f("code"), 1.0, A.is_le)
        ms(f("ones"), 1.0)
        ts(f("zc3"), f("rp"), 16.0, A.mult)
        ts(f("J16"), f("j16"), f("zc3"), A.add)
        ts(f("c613"), f("rp"), 613.0, A.mult, -15.5 / 32, A.add)
        ts(f("bG"), f("rp"), -1.0, A.mult, 0.5, A.add)
        tt(f("bY"), f("bG"), f("m15"), A.add)
        ts(f("bM"), f("rp"), -1.5, A.mult)
        ts(f("Tn"), f("tI"), -1.0, A.mult, -0.5, A.add)
        ts(f("Tp"), f("tI"), 0.5, A.add)
        cp(f("thr"), f("Tn"))

    def keys_t(prods, pb, null=False):
        for h in range(2):
            if null:
                mm(f(pb, 128, 128 * h), f("ones", 128), f("cSq"), True, False)
            for i, (rows, sel, nsel) in enumerate(prods):
                mm(f(pb, 128, 128 * h), f(rows, 128, 128 * h), f(sel), i == 0 and not null, i == len(prods) - 1)

    def diff(prods, wt, pb):
        mm(f(pb, 256, 256), f("cI"), f("MSK"), True, False)
        for rows, sel, nsel in prods:
            mm(f(pb, 256, 256), f(nsel), f(rows), False, False)
        for h in range(2):
            mm(f(pb, 128, 256 + 128 * h), f(wt, 128, 128 * h), f("cS"), False, h == 1)

    def mylist(wt, pb, a, stop):
        for h in range(2):
            mm(f(pb, 16, a), f(wt, 128, 128 * h), f("dd", 16, 16 * h), h == 0, stop and h == 1)

    def lost(em, pb):
        for r in range(16):
            mm(f(pb, 16), sk(r), (em, r, K, 16), False, r == 15)

    def eqs(em, pb, null=0.0):
        ts(f(em), f(pb, 256, 256), null, A.is_equal, -8192.0, A.mult)

    def offs(of, pb, c):
        ts((of, 0, 31, 2), f(pb, 16), c, A.add, f("rp"), A.max)

    def scatter(tab, of, data):
        for s in range(15, -1, -1):
            cp(("@", f(tab), (of, 2 * s, 2 * s + 1)), f(data, 16, 16 * s))

    FW, XW = f("Fw", W, PAD), f("X", W, PAD)
    pb = [("bu", "cSb", "cSbn")]
    pw = [("Vw", "cS", "cSn")]
    ph = [("Vh", "cS", "cSn"), ("mg", "cS4", "cS4n")]

    def pf(c):
        return 512 * (c % 2) + CL * (c // 2)

    def turn(out, src, c, stop=True):
        for k in range(LV):
            mm(out, sk(k), (src, CE * c + k, CE * (c + 1), LV), k == 0, stop and k == LV - 1)

    def step(s, v, L, z, last, dst):
        c = int(s[2]) if len(s) == 3 and s[2] in "0123" else 0
        zs, nx = "zs%d" % (v + 1), "%d" % (v + 1)
        lanes, ents = CL * c, f("z16", CE, CE * c)
        k = s[:2]
        if k == "fg":
            act(f("FG", CE, CE * c), ("@", FW, f(L, CL, lanes)), AF.Copy)
        elif k == "fh":
            act(f("FH", CE, CE * c), ("@", FW, f("Bb", CL, lanes)), AF.Copy)
        elif k == "zb":
            mm(f("pX", 256), f("cZ"), f(z))
            ts(f("i1"), f("pX", 256), 255.0, A.add)
            ts(f("i2"), f("i1"), 1023, A.bitwise_and)
            cp(f("bu"), f("i2"))
            keys_t(pb, "pC")
            cp(("zsp", 0, W, LV), f(z))
            tt(f("WTb"), f("pC", 256), f("mask"), A.mult)
            mylist("WTb", "pC", 16, True)
            cp(f("bl"), f("pC", 16, 16))
            cp(f("Bb"), ("@", f("Bt", C, PAD), f("bl")))
            diff(pb, "WTb", "pC")
            mm(f("pX", 256, 256), f("cS1"), f("bu"))
        elif k == "sc":
            for c in range(NCH):
                scan(f("z16", CE, CE * c), f("zm", CE, CE * c), f("zsp", CE, CE * c), A.mult, A.add)
        elif k == "eb":
            eqs("Emb", "pC")
        elif k == "ob":
            mylist("WTb", "pC", 0, False)
            lost("Emb", "pC")
            offs("ofb", "pC", float(PAD))
        elif s == "flf":
            act(f("FLf"), f("FLc"), AF.Identity, 2048.0)
            if v == 0:
                late_constants()
        elif k == "xl":
            turn(f("pF", CL, pf(c)), "FG", c)
        elif k == "ul":
            ts(f("FLu", CL, lanes), f("pF", CL, pf(c)), 2048.0, A.add)
            cp(f("FLc", CL, lanes), f("pF", CL, pf(c)))
            tt(f("D", CE, CE * c), ("@", XW, f("FLu", CL, lanes)), ents, A.subtract)
        elif k == "xg":
            turn(f("pF", CL, pf(NCH + c)), "FH", c)
        elif k == "ug":
            p = f("pF", CL, pf(NCH + c))
            ts(f("Gu", CL, lanes), p, 2048.0, A.add)
            tt(f("eq", CL, lanes), p, f("FLc", CL, lanes), A.is_equal)
            tt(f("pH", CL, lanes), p, f("FLc", CL, lanes), A.max)
            tt(f("pH", CL, 256 + lanes), p, f("FLc", CL, lanes), A.min)
            tt(f("E", CE, CE * c), ("@", XW, f("Gu", CL, lanes)), ents, A.subtract)
        elif k == "da":
            act(f("DA", CE, CE * c), f("D", CE, CE * c), AF.Abs)
        elif k == "sd":
            turn(f("pd", CL, lanes), "DA", c)
        elif k == "ea":
            act(f("EA", CE, CE * c), f("E", CE, CE * c), AF.Abs)
        elif k == "se":
            turn(f("pe", CL, lanes), "EA", c, False)
            mm(f("pe", CL, lanes), f("cI8"), f("eq", CL, lanes), False, True)
        elif k == "df":
            act(f("fs"), f("pd", 256), AF.Sign, f("thr"))
            mm(f("pC", 256), f("C1"), f("ones"), True, False)
            mm(f("pC", 256), f("C1"), f("fs"), False, True)
            mm(f("pd", 256, 256), f("C2f"), f("fs"))
            act(f("pd", 256), f("pd", 256, 256), AF.Relu, f("bY"))
        elif k == "nn":
            mm(f("pd", 256, 256), f("C4"), f("fs"))
            act(f("pd", 256, 256), f("pd", 256, 256), AF.Relu, -7.0)
        elif k == "nw":
            tt(f("r1"), f("pX", 256, 256), f("FLf"), A.mult)
            ts(f("r2"), f("r1"), f("c613"), A.add)
            tt(f("pC", 256, 256), f("pC", 256), f("r2"), A.min)
            tt(f("sn"), f("pC", 256, 256), f("FLf"), A.add)
            ts(f("new"), f("sn"), 4095, A.bitwise_and)
        elif k == "sl":
            if last:
                cp(f("ylo"), f("new"))
                dma("y", T.yl[:, :], T.ylo[:, :], [f("ylo")], [])
            else:
                cp(f("Ls" + nx), f("new"))
                send(f("Ls" + nx), f("L" + nx), topo, core, dst, "aL" + nx, "lL" + nx, "L" + nx)
        elif k == "wv":
            ts(f("nC"), f("new"), -2048.0, A.add)
            tt(f("Vw"), f("pd", 256), f("nC"), A.mult)
        elif k == "wm":
            keys_t(pw, "pX")
            tt(f("WTw"), f("pX", 256), f("mask"), A.mult)
            diff(pw, "WTw", "pX")
            mylist("WTw", "pX", 0, False)
        elif k == "we":
            eqs("Emw", "pX")
        elif k == "wl":
            lost("Emw", "pX")
        elif k == "wo":
            offs("ofw", "pX", float(2048 + PAD))
        elif k == "eg":
            act(f("gs"), f("pe", 256), AF.Sign, f("Tp"), -1.0)
            mm(f("pS", 256, 256), f("C3"), f("fs"), True, False)
            mm(f("pS", 256, 256), f("C2"), f("gs"), False, True)
            act(f("mg"), f("pS", 256, 256), AF.Relu, f("bM"), 1.0, f("Aac"))
            mm(f("pS", 256), f("C2"), f("gs"))
            act(f("fg"), f("pS", 256), AF.Relu, f("bG"))
        elif k == "h1":
            tt(f("Vh"), f("pH", 256), f("mg"), A.mult)
        elif k == "hk":
            keys_t(ph, "pC", True)
        elif k == "zi":
            mm(f("pF", 16, 256), f("cI"), f("J16"), True, False)
            for r in range(16):
                mm(f("pF", 16, 256), sk(r, "MK"), ("fg", r, K, 16), False, r == 15)
            mm(f("pF", 256), f("cS"), f("fg"))
        elif k == "zz":
            cp(f("idx"), f("pF", 16, 256))
            ts(f("zh"), ("@", f("E"), f("idx")), 0.5, A.mult, -0.25, A.add)
            tt(f("pF", 256, 256), f("pF", 256), f("zh"), A.mult)
            tt(f(zs), f("pF", 256, 256), f(z), A.add)
            if last:
                dma("y", T.yz[:, :], T[zs][:, :], [f(zs)], [])
            else:
                send(f(zs), f("z" + nx), topo, core, dst, "aZ" + nx, "lZ" + nx, "Z" + nx)
        elif k == "h2":
            tt(f("WTh"), f("pC", 256), f("mask"), A.mult)
            diff(ph, "WTh", "pC")
            mylist("WTh", "pC", 0, False)
        elif k == "h3":
            eqs("Emh", "pC", -4096.0)
            lost("Emh", "pC")
        elif k == "h4":
            offs("ofh", "pC", float(PAD + 2048))
        elif k == "l1":
            tt(f("Vl"), f("pH", 256, 256), f("mg"), A.mult)
        elif k == "lm":
            mm(f("pF", 256, 768), f("c01"), f("Vl"))
            if last:
                ts(f("lof"), f("pF", 256, 768), 2048.0, A.add)
            else:
                act(f("hm"), f("pF", 256, 768), AF.Identity, 0.0, f("m0"))
        elif k == "l2":
            tt(f("lod"), f("pF", 256, 768), f("hm"), A.subtract)
        elif k == "ff":
            for b in (2 * c, 2 * c + 1):
                bank = ("pd", "pX")[b % 2]
                mm(f(bank), f("cS"), f("Fw", 512, PAD + 512 * b))
                act(f("Ff", 512, PAD + 512 * b), f(bank), AF.Identity, 2048.0)
        elif k == "fs":
            if last:
                scatter("Ff", "ofh", "lof")
                dma("y", T.yf[:, :], T.Ff[0:128:16, PAD:PAD + W], [f("Ff")], [])
            else:
                scatter("Fw", "ofh", "lod")
        elif k == "bs":
            scatter("Bt", "ofb", "new")
            if last:
                cp(f("ybo"), f("Bt", C, PAD))
                dma("y", T.yb[:, :], T.ybo[:, :], [f("ybo")], [], False, 4.5)
        elif k == "hv":
            ts(f("hd"), ("D", 15, W, LV), 0.5, A.mult, -0.25, A.add)
        elif k == "vv":
            tt(f("pd", 256, 256), f("pd", 256, 256), f("hd"), A.mult)
            tt(f("val"), f("pd", 256, 256), f(z), A.add)
        elif k == "xs":
            scatter("X", "ofw", "val")
            if last:
                dma("s", T.yx[:, :], T.X[:, PAD:PAD + W], [f("X", W, PAD)], [], False, 7.0)
        elif k == "aa":
            mm(f("pS", 1, 256), f("cSf"), f("Aac"))
            cp(f("a1"), f("pS", 1, 256))
            ts(f("a2"), f("a1"), 15, A.bitwise_and)
            tt(f("thr"), f("Tn"), f("a2"), A.subtract)

    for v in range(VIS):
        L, z = "L%d" % v, "z%d" % v
        last = v == VIS - 1
        dst = T.cores[(rank + 1 + v % (ranks - 1)) % ranks]
        if v > 0:
            src = T.cores[(rank - 1 - (v - 1) % (ranks - 1)) % ranks]
            n = len(topo.engines(src, core))
            arrive(f(L), "aL%d" % v, n, "L%d" % v)
            arrive(f(z), "aZ%d" % v, n, "Z%d" % v)
        for s in (ORDER_LAST if last else ORDER).split():
            step(s, v, L, z, last, dst)
    issue()
